import numpy as np
import ml_dtypes

BF16 = ml_dtypes.bfloat16


def bf(x):
    return np.asarray(x, np.float32).astype(BF16)


def f32(x):
    return np.asarray(x, np.float32)


def f64(x):
    return np.asarray(x).astype(np.float64)


def striped(idx):
    return np.tile(idx.reshape(-1, 16).T, (8, 1))


S, K, M, N, V, D = 512, 256, 512, 64, 8, 64


def setup_inputs():
    return {"base": bf(np.random.standard_normal((M, S))), "x": bf(np.random.standard_normal((K, N))), "w": bf(1.5 * np.random.standard_normal((K, M)) / np.sqrt(K)), "s": f32(0.5 + np.random.random_sample((M, 1))), "offs": striped(np.random.permutation(S)[:N])}


def reference(base, x, w, s, offs):
    idx = offs[:16].T.reshape(-1)
    z = f64(base).copy()
    z[:, idx] += f64(w).T @ f64(x)
    z = z * f64(s)
    u = z.reshape(M, V, D)
    u = u - u.max(axis=2, keepdims=True)
    u = np.exp(u)
    u = u / u.sum(axis=2, keepdims=True)
    return u.reshape(M, S)

@@ -1,0 +1,72 @@
+import concourse.mybir as mybir
+from concourse.masks import make_identity
+
+BF16, F32, U16 = mybir.dt.bfloat16, mybir.dt.float32, mybir.dt.uint16
+COPY = mybir.ActivationFunctionType.Copy
+EXP = mybir.ActivationFunctionType.Exp
+MULT, SUBTRACT = mybir.AluOpType.mult, mybir.AluOpType.subtract
+AX = mybir.AxisListType.X
+
+P = 128
+S = 512
+K = 256
+M = 512
+N = 64
+V, D = 8, 64
+WINDOWS = M // P
+BLOCKS = K // P
+
+FLOPS = 2 * K * M * N
+
+
+def tile_rows_rescore_kernel(tc, base, x, w, s, offs, out):
+    nc = tc.nc
+    with (
+        tc.tile_pool(name="held", bufs=1) as held,
+        tc.tile_pool(name="work", bufs=2) as work,
+        tc.psum_pool(name="psum", bufs=1) as psum,
+    ):
+        offsets = held.tile([P, N // 16], U16, name="offsets")
+        base_t = held.tile([P, WINDOWS, S], BF16, name="base_t")
+        w_t = held.tile([P, BLOCKS, M], BF16, name="w_t")
+        x_t = held.tile([P, BLOCKS, N], BF16, name="x_t")
+        s_t = held.tile([P, WINDOWS], F32, name="s_t")
+        ident = held.tile([P, P], BF16, name="ident")
+
+        nc.sync.dma_start(base_t[:], base.rearrange("(a p) i -> p a i", p=P))
+        nc.sync.dma_start(offsets[:], offs)
+        nc.scalar.dma_start(w_t[:], w.rearrange("(p b) m -> p b m", b=BLOCKS))
+        nc.scalar.dma_start(x_t[:], x.rearrange("(p b) j -> p b j", b=BLOCKS))
+        nc.scalar.dma_start(s_t[:], s.rearrange("(a p) o -> p (a o)", p=P))
+        make_identity(nc, ident[:])
+
+        windows = [psum.tile([P, S], F32, name=f"window{a}") for a in range(WINDOWS)]
+        for a in range(WINDOWS):
+            nc.tensor.matmul(windows[a][:], ident[:], base_t[:, a, :], start=True, stop=False)
+        for a in range(WINDOWS):
+            for b in range(BLOCKS):
+                nc.tensor.matmul(
+                    windows[a][:].indirect(offsets[:]),
+                    w_t[:, b, a * P : (a + 1) * P],
+                    x_t[:, b, :],
+                    start=False,
+                    stop=b == BLOCKS - 1,
+                )
+
+        for a in range(WINDOWS):
+            t = work.tile([P, V, D], F32, name="t")
+            top = work.tile([P, V], F32, name="top")
+            u = work.tile([P, V, D], F32, name="u")
+            e = work.tile([P, V, D], F32, name="e")
+            total = work.tile([P, V], F32, name="total")
+            inverse = work.tile([P, V], F32, name="inverse")
+            y = work.tile([P, V, D], F32, name="y")
+            slates = windows[a][:].rearrange("p (v d) -> p v d", v=V)
+            nc.scalar.activation(t[:], slates, COPY, scale=s_t[:, a : a + 1])
+            nc.vector.reduce_max(top[:], t[:], axis=AX)
+            nc.vector.tensor_tensor(u[:], t[:], top[:].unsqueeze(2).to_broadcast([P, V, D]), SUBTRACT)
+            nc.scalar.activation(e[:], u[:], EXP)
+            nc.vector.reduce_sum(total[:], e[:], axis=AX)
+            nc.vector.reciprocal(inverse[:], total[:])
+            nc.vector.tensor_tensor(y[:], e[:], inverse[:].unsqueeze(2).to_broadcast([P, V, D]), MULT)
+            nc.sync.dma_start(out[a * P : (a + 1) * P, :], y[:].rearrange("p v d -> p (v d)"))

@@ -4,7 +4,7 @@ from concourse.masks import make_identity
 BF16, F32, U16 = mybir.dt.bfloat16, mybir.dt.float32, mybir.dt.uint16
 COPY = mybir.ActivationFunctionType.Copy
 EXP = mybir.ActivationFunctionType.Exp
-MULT, SUBTRACT = mybir.AluOpType.mult, mybir.AluOpType.subtract
+MULT, MAX = mybir.AluOpType.mult, mybir.AluOpType.max
 AX = mybir.AxisListType.X
 
 P = 128
@@ -23,7 +23,7 @@ def tile_rows_rescore_kernel(tc, base, x, w, s, offs, out):
     nc = tc.nc
     with (
         tc.tile_pool(name="held", bufs=1) as held,
-        tc.tile_pool(name="work", bufs=2) as work,
+        tc.tile_pool(name="work", bufs=4) as work,
         tc.psum_pool(name="psum", bufs=1) as psum,
     ):
         offsets = held.tile([P, N // 16], U16, name="offsets")
@@ -33,11 +33,19 @@ def tile_rows_rescore_kernel(tc, base, x, w, s, offs, out):
         s_t = held.tile([P, WINDOWS], F32, name="s_t")
         ident = held.tile([P, P], BF16, name="ident")
 
-        nc.sync.dma_start(base_t[:], base.rearrange("(a p) i -> p a i", p=P))
-        nc.sync.dma_start(offsets[:], offs)
+        base_rows = base.rearrange("(p a) i -> p a i", a=WINDOWS)
+        out_rows = out.rearrange("(p a) i -> p a i", a=WINDOWS)
+        for a in range(WINDOWS):
+            nc.sync.dma_start(base_t[:, a, :], base_rows[:, a, :])
         nc.scalar.dma_start(w_t[:], w.rearrange("(p b) m -> p b m", b=BLOCKS))
         nc.scalar.dma_start(x_t[:], x.rearrange("(p b) j -> p b j", b=BLOCKS))
-        nc.scalar.dma_start(s_t[:], s.rearrange("(a p) o -> p (a o)", p=P))
+        nc.sync.dma_start(offsets[:], offs)
+        nc.scalar.dma_start(s_t[:], s.rearrange("(p a) o -> p (a o)", a=WINDOWS))
+
+        zero = held.tile([P, 1], F32, name="zero")
+        one = held.tile([P, 1], F32, name="one")
+        nc.vector.memset(zero[:], 0.0)
+        nc.scalar.activation(one[:], zero[:], EXP)
         make_identity(nc, ident[:])
 
         windows = [psum.tile([P, S], F32, name=f"window{a}") for a in range(WINDOWS)]
@@ -47,7 +55,7 @@ def tile_rows_rescore_kernel(tc, base, x, w, s, offs, out):
             for b in range(BLOCKS):
                 nc.tensor.matmul(
                     windows[a][:].indirect(offsets[:]),
-                    w_t[:, b, a * P : (a + 1) * P],
+                    w_t[:, b, a::WINDOWS],
                     x_t[:, b, :],
                     start=False,
                     stop=b == BLOCKS - 1,
@@ -55,18 +63,18 @@ def tile_rows_rescore_kernel(tc, base, x, w, s, offs, out):
 
         for a in range(WINDOWS):
             t = work.tile([P, V, D], F32, name="t")
-            top = work.tile([P, V], F32, name="top")
-            u = work.tile([P, V, D], F32, name="u")
+            negtop = work.tile([P, V], F32, name="negtop")
             e = work.tile([P, V, D], F32, name="e")
             total = work.tile([P, V], F32, name="total")
             inverse = work.tile([P, V], F32, name="inverse")
             y = work.tile([P, V, D], F32, name="y")
             slates = windows[a][:].rearrange("p (v d) -> p v d", v=V)
             nc.scalar.activation(t[:], slates, COPY, scale=s_t[:, a : a + 1])
-            nc.vector.reduce_max(top[:], t[:], axis=AX)
-            nc.vector.tensor_tensor(u[:], t[:], top[:].unsqueeze(2).to_broadcast([P, V, D]), SUBTRACT)
-            nc.scalar.activation(e[:], u[:], EXP)
+            nc.vector.tensor_reduce(negtop[:], t[:], axis=AX, op=MAX, negate=True)
+            for v in range(V):
+                nc.scalar.activation(e[:, v, :], t[:, v, :], EXP, bias=negtop[:, v : v + 1])
             nc.vector.reduce_sum(total[:], e[:], axis=AX)
             nc.vector.reciprocal(inverse[:], total[:])
-            nc.vector.tensor_tensor(y[:], e[:], inverse[:].unsqueeze(2).to_broadcast([P, V, D]), MULT)
-            nc.sync.dma_start(out[a * P : (a + 1) * P, :], y[:].rearrange("p v d -> p (v d)"))
+            normaliser = nc.gpsimd if a % 2 == 0 else nc.vector
+            normaliser.tensor_tensor(y[:], e[:], inverse[:].unsqueeze(2).to_broadcast([P, V, D]), MULT)
+            nc.sync.dma_start(out_rows[:, a, :], y[:].rearrange("p v d -> p (v d)"))

@@ -15,6 +15,7 @@ N = 64
 V, D = 8, 64
 WINDOWS = M // P
 BLOCKS = K // P
+WARM_UPS = 4
 
 FLOPS = 2 * K * M * N
 
@@ -48,6 +49,12 @@ def tile_rows_rescore_kernel(tc, base, x, w, s, offs, out):
         nc.scalar.activation(one[:], zero[:], EXP)
         make_identity(nc, ident[:])
 
+        zeros = held.tile([P, S], BF16, name="zeros")
+        spare = psum.tile([P, S], F32, name="spare")
+        nc.vector.memset(zeros[:], 0.0)
+        for step in range(WARM_UPS):
+            nc.tensor.matmul(spare[:], zeros[:, 0:P], zeros[:], start=True, stop=True)
+
         windows = [psum.tile([P, S], F32, name=f"window{a}") for a in range(WINDOWS)]
         for a in range(WINDOWS):
             nc.tensor.matmul(windows[a][:], ident[:], base_t[:, a, :], start=True, stop=False)
@@ -65,16 +72,20 @@ def tile_rows_rescore_kernel(tc, base, x, w, s, offs, out):
             t = work.tile([P, V, D], F32, name="t")
             negtop = work.tile([P, V], F32, name="negtop")
             e = work.tile([P, V, D], F32, name="e")
-            total = work.tile([P, V], F32, name="total")
-            inverse = work.tile([P, V], F32, name="inverse")
-            y = work.tile([P, V, D], F32, name="y")
             slates = windows[a][:].rearrange("p (v d) -> p v d", v=V)
             nc.scalar.activation(t[:], slates, COPY, scale=s_t[:, a : a + 1])
             nc.vector.tensor_reduce(negtop[:], t[:], axis=AX, op=MAX, negate=True)
             for v in range(V):
                 nc.scalar.activation(e[:, v, :], t[:, v, :], EXP, bias=negtop[:, v : v + 1])
-            nc.vector.reduce_sum(total[:], e[:], axis=AX)
-            nc.vector.reciprocal(inverse[:], total[:])
             normaliser = nc.gpsimd if a % 2 == 0 else nc.vector
-            normaliser.tensor_tensor(y[:], e[:], inverse[:].unsqueeze(2).to_broadcast([P, V, D]), MULT)
-            nc.sync.dma_start(out_rows[:, a, :], y[:].rearrange("p v d -> p (v d)"))
+            parts = 2 if a == WINDOWS - 1 else 1
+            wide = V // parts
+            for h in range(parts):
+                total = work.tile([P, wide], F32, name=f"total{a}_{h}")
+                inverse = work.tile([P, wide], F32, name=f"inverse{a}_{h}")
+                y = work.tile([P, wide, D], F32, name=f"y{a}_{h}")
+                part = e[:, h * wide : (h + 1) * wide, :]
+                nc.vector.reduce_sum(total[:], part, axis=AX)
+                nc.vector.reciprocal(inverse[:], total[:])
+                normaliser.tensor_tensor(y[:], part, inverse[:].unsqueeze(2).to_broadcast([P, wide, D]), MULT)
+                nc.sync.dma_start(out_rows[:, a, h * wide * D : (h + 1) * wide * D], y[:].rearrange("p v d -> p (v d)"))

@@ -15,7 +15,7 @@ N = 64
 V, D = 8, 64
 WINDOWS = M // P
 BLOCKS = K // P
-WARM_UPS = 4
+WARM_UPS = 3
 
 FLOPS = 2 * K * M * N
 
@@ -42,16 +42,13 @@ def tile_rows_rescore_kernel(tc, base, x, w, s, offs, out):
         nc.scalar.dma_start(x_t[:], x.rearrange("(p b) j -> p b j", b=BLOCKS))
         nc.sync.dma_start(offsets[:], offs)
         nc.scalar.dma_start(s_t[:], s.rearrange("(p a) o -> p (a o)", a=WINDOWS))
-
-        zero = held.tile([P, 1], F32, name="zero")
-        one = held.tile([P, 1], F32, name="one")
-        nc.vector.memset(zero[:], 0.0)
-        nc.scalar.activation(one[:], zero[:], EXP)
         make_identity(nc, ident[:])
 
         zeros = held.tile([P, S], BF16, name="zeros")
+        one = held.tile([P, 1], F32, name="one")
         spare = psum.tile([P, S], F32, name="spare")
         nc.vector.memset(zeros[:], 0.0)
+        nc.scalar.activation(one[:], zeros[:, 0:1], EXP)
         for step in range(WARM_UPS):
             nc.tensor.matmul(spare[:], zeros[:, 0:P], zeros[:], start=True, stop=True)
 
@@ -72,20 +69,20 @@ def tile_rows_rescore_kernel(tc, base, x, w, s, offs, out):
             t = work.tile([P, V, D], F32, name="t")
             negtop = work.tile([P, V], F32, name="negtop")
             e = work.tile([P, V, D], F32, name="e")
+            total = work.tile([P, V], F32, name="total")
+            inverse = work.tile([P, V], F32, name="inverse")
             slates = windows[a][:].rearrange("p (v d) -> p v d", v=V)
             nc.scalar.activation(t[:], slates, COPY, scale=s_t[:, a : a + 1])
             nc.vector.tensor_reduce(negtop[:], t[:], axis=AX, op=MAX, negate=True)
             for v in range(V):
-                nc.scalar.activation(e[:, v, :], t[:, v, :], EXP, bias=negtop[:, v : v + 1])
-            normaliser = nc.gpsimd if a % 2 == 0 else nc.vector
+                nc.scalar.activation(e[:, v, :], t[:, v, :], EXP, bias=negtop[:, v : v + 1], accum_out=total[:, v : v + 1])
+            normaliser = nc.vector
             parts = 2 if a == WINDOWS - 1 else 1
             wide = V // parts
             for h in range(parts):
-                total = work.tile([P, wide], F32, name=f"total{a}_{h}")
-                inverse = work.tile([P, wide], F32, name=f"inverse{a}_{h}")
-                y = work.tile([P, wide, D], F32, name=f"y{a}_{h}")
-                part = e[:, h * wide : (h + 1) * wide, :]
-                nc.vector.reduce_sum(total[:], part, axis=AX)
-                nc.vector.reciprocal(inverse[:], total[:])
-                normaliser.tensor_tensor(y[:], part, inverse[:].unsqueeze(2).to_broadcast([P, wide, D]), MULT)
+                these = slice(h * wide, (h + 1) * wide)
+                y = work.tile([P, wide, D], F32, name=f"y{parts}_{h}")
+                nc.vector.reciprocal(inverse[:, these], total[:, these])
+                inverses = inverse[:, these].unsqueeze(2).to_broadcast([P, wide, D])
+                normaliser.tensor_tensor(y[:], e[:, these, :], inverses, MULT)
                 nc.sync.dma_start(out_rows[:, a, h * wide * D : (h + 1) * wide * D], y[:].rearrange("p v d -> p (v d)"))

@@ -5,7 +5,7 @@ BF16, F32, U16 = mybir.dt.bfloat16, mybir.dt.float32, mybir.dt.uint16
 COPY = mybir.ActivationFunctionType.Copy
 EXP = mybir.ActivationFunctionType.Exp
 MULT, MAX = mybir.AluOpType.mult, mybir.AluOpType.max
-AX = mybir.AxisListType.X
+FREE_AXIS = mybir.AxisListType.X
 
 P = 128
 S = 512
@@ -24,7 +24,7 @@ def tile_rows_rescore_kernel(tc, base, x, w, s, offs, out):
     nc = tc.nc
     with (
         tc.tile_pool(name="held", bufs=1) as held,
-        tc.tile_pool(name="work", bufs=4) as work,
+        tc.tile_pool(name="work", bufs=WINDOWS) as work,
         tc.psum_pool(name="psum", bufs=1) as psum,
     ):
         offsets = held.tile([P, N // 16], U16, name="offsets")
@@ -71,12 +71,20 @@ def tile_rows_rescore_kernel(tc, base, x, w, s, offs, out):
             e = work.tile([P, V, D], F32, name="e")
             total = work.tile([P, V], F32, name="total")
             inverse = work.tile([P, V], F32, name="inverse")
-            slates = windows[a][:].rearrange("p (v d) -> p v d", v=V)
-            nc.scalar.activation(t[:], slates, COPY, scale=s_t[:, a : a + 1])
-            nc.vector.tensor_reduce(negtop[:], t[:], axis=AX, op=MAX, negate=True)
+
+            z = windows[a][:].rearrange("p (v d) -> p v d", v=V)
+            if a == 1:
+                nc.vector.tensor_scalar(t[:], z, s_t[:, a : a + 1], None, op0=MULT)
+            else:
+                nc.scalar.activation(t[:], z, COPY, scale=s_t[:, a : a + 1])
+
+            nc.vector.tensor_reduce(negtop[:], t[:], axis=FREE_AXIS, op=MAX, negate=True)
             for v in range(V):
-                nc.scalar.activation(e[:, v, :], t[:, v, :], EXP, bias=negtop[:, v : v + 1], accum_out=total[:, v : v + 1])
-            normaliser = nc.vector
+                nc.scalar.activation(
+                    e[:, v, :], t[:, v, :], EXP, bias=negtop[:, v : v + 1], accum_out=total[:, v : v + 1]
+                )
+
+            normaliser = nc.gpsimd if a == 0 else nc.vector
             parts = 2 if a == WINDOWS - 1 else 1
             wide = V // parts
             for h in range(parts):
@@ -85,4 +93,6 @@ def tile_rows_rescore_kernel(tc, base, x, w, s, offs, out):
                 nc.vector.reciprocal(inverse[:, these], total[:, these])
                 inverses = inverse[:, these].unsqueeze(2).to_broadcast([P, wide, D])
                 normaliser.tensor_tensor(y[:], e[:, these, :], inverses, MULT)
-                nc.sync.dma_start(out_rows[:, a, h * wide * D : (h + 1) * wide * D], y[:].rearrange("p v d -> p (v d)"))
+                nc.sync.dma_start(
+                    out_rows[:, a, h * wide * D : (h + 1) * wide * D], y[:].rearrange("p v d -> p (v d)")
+                )

import concourse.mybir as mybir
from concourse.masks import make_identity

BF16, F32, U16 = mybir.dt.bfloat16, mybir.dt.float32, mybir.dt.uint16
COPY = mybir.ActivationFunctionType.Copy
EXP = mybir.ActivationFunctionType.Exp
MULT, MAX = mybir.AluOpType.mult, mybir.AluOpType.max
FREE_AXIS = mybir.AxisListType.X

P = 128
S = 512
K = 256
M = 512
N = 64
V, D = 8, 64
WINDOWS = M // P
BLOCKS = K // P
WARM_UPS = 3

FLOPS = 2 * K * M * N


def tile_rows_rescore_kernel(tc, base, x, w, s, offs, out):
    nc = tc.nc
    with (
        tc.tile_pool(name="held", bufs=1) as held,
        tc.tile_pool(name="work", bufs=WINDOWS) as work,
        tc.psum_pool(name="psum", bufs=1) as psum,
    ):
        offsets = held.tile([P, N // 16], U16, name="offsets")
        base_t = held.tile([P, WINDOWS, S], BF16, name="base_t")
        w_t = held.tile([P, BLOCKS, M], BF16, name="w_t")
        x_t = held.tile([P, BLOCKS, N], BF16, name="x_t")
        s_t = held.tile([P, WINDOWS], F32, name="s_t")
        ident = held.tile([P, P], BF16, name="ident")

        base_rows = base.rearrange("(p a) i -> p a i", a=WINDOWS)
        out_rows = out.rearrange("(p a) i -> p a i", a=WINDOWS)
        for a in range(WINDOWS):
            nc.sync.dma_start(base_t[:, a, :], base_rows[:, a, :])
        nc.scalar.dma_start(w_t[:], w.rearrange("(p b) m -> p b m", b=BLOCKS))
        nc.scalar.dma_start(x_t[:], x.rearrange("(p b) j -> p b j", b=BLOCKS))
        nc.sync.dma_start(offsets[:], offs)
        nc.scalar.dma_start(s_t[:], s.rearrange("(p a) o -> p (a o)", a=WINDOWS))
        make_identity(nc, ident[:])

        zeros = held.tile([P, S], BF16, name="zeros")
        one = held.tile([P, 1], F32, name="one")
        spare = psum.tile([P, S], F32, name="spare")
        nc.vector.memset(zeros[:], 0.0)
        nc.scalar.activation(one[:], zeros[:, 0:1], EXP)
        for step in range(WARM_UPS):
            nc.tensor.matmul(spare[:], zeros[:, 0:P], zeros[:], start=True, stop=True)

        windows = [psum.tile([P, S], F32, name=f"window{a}") for a in range(WINDOWS)]
        for a in range(WINDOWS):
            nc.tensor.matmul(windows[a][:], ident[:], base_t[:, a, :], start=True, stop=False)
        for a in range(WINDOWS):
            for b in range(BLOCKS):
                nc.tensor.matmul(
                    windows[a][:].indirect(offsets[:]),
                    w_t[:, b, a::WINDOWS],
                    x_t[:, b, :],
                    start=False,
                    stop=b == BLOCKS - 1,
                )

        for a in range(WINDOWS):
            t = work.tile([P, V, D], F32, name="t")
            negtop = work.tile([P, V], F32, name="negtop")
            e = work.tile([P, V, D], F32, name="e")
            total = work.tile([P, V], F32, name="total")
            inverse = work.tile([P, V], F32, name="inverse")

            z = windows[a][:].rearrange("p (v d) -> p v d", v=V)
            if a == 1:
                nc.vector.tensor_scalar(t[:], z, s_t[:, a : a + 1], None, op0=MULT)
            else:
                nc.scalar.activation(t[:], z, COPY, scale=s_t[:, a : a + 1])

            nc.vector.tensor_reduce(negtop[:], t[:], axis=FREE_AXIS, op=MAX, negate=True)
            for v in range(V):
                nc.scalar.activation(
                    e[:, v, :], t[:, v, :], EXP, bias=negtop[:, v : v + 1], accum_out=total[:, v : v + 1]
                )

            normaliser = nc.gpsimd if a == 0 else nc.vector
            parts = 2 if a == WINDOWS - 1 else 1
            wide = V // parts
            for h in range(parts):
                these = slice(h * wide, (h + 1) * wide)
                y = work.tile([P, wide, D], F32, name=f"y{parts}_{h}")
                nc.vector.reciprocal(inverse[:, these], total[:, these])
                inverses = inverse[:, these].unsqueeze(2).to_broadcast([P, wide, D])
                normaliser.tensor_tensor(y[:], e[:, these, :], inverses, MULT)
                nc.sync.dma_start(
                    out_rows[:, a, h * wide * D : (h + 1) * wide * D], y[:].rearrange("p v d -> p (v d)")
                )
